import numpy as np
import ml_dtypes


def mxq(x, axis, fmt="e4m3"):
    dtype, down = {"e4m3": (ml_dtypes.float8_e4m3fn, 7), "e5m2": (ml_dtypes.float8_e5m2, 14)}[fmt]
    v = np.moveaxis(np.asarray(x, np.float32).astype(ml_dtypes.bfloat16).astype(np.float64), axis, -1)
    blocks = v.reshape(v.shape[:-1] + (-1, 32))
    amax = np.abs(blocks).max(-1, keepdims=True)
    byte = np.maximum(np.where(amax > 0, np.frexp(amax)[1] - 1 + 127, 0) - down, 1)
    scale = np.exp2(byte - 127.0)
    codes = (blocks / scale).astype(np.float32).astype(dtype).astype(np.float64)
    return np.moveaxis((codes * scale).reshape(v.shape), -1, axis)


WIDE = False


def mx_kscale(k):
    if not WIDE:
        return np.ones(k)
    levels = np.array([10, -10, 5, -5, 0])
    if k % 512:
        return np.exp2(np.random.permutation(np.resize(levels, k // 32))).repeat(32)
    a = np.empty((k // 512, 16))
    for p in range(k // 512):
        a[p, :8] = np.random.permutation(np.resize(levels, 8))
        for g in range(8):
            far = levels[np.abs(levels - a[p, g]) >= 10]
            a[p, g + 8] = far[np.random.randint(len(far))]
    return np.exp2(a.ravel()).repeat(32)


def f64(x):
    return np.asarray(x).astype(np.float64)


def striped(idx):
    return np.tile(idx.reshape(-1, 16).T, (8, 1)).astype(np.uint16)


def unstriped(offs):
    return offs[:16].T.reshape(-1).astype(np.int64)


def pack_weight(w):
    k, n = w.shape
    w = f64(np.asarray(w, np.float32).astype(ml_dtypes.bfloat16)).reshape(k // 32, 32, n)
    amax = np.abs(w).max(1)
    byte = np.clip(np.where(amax > 0, np.frexp(amax)[1] - 1 + 127 - 7, 1), 1, 254)
    scaled = (w * np.exp2(127.0 - byte)[:, None, :]).reshape(k, n).astype(np.float32)
    words = np.ascontiguousarray(scaled.reshape(k // 512, 128, 4, n).transpose(0, 1, 3, 2)).astype(ml_dtypes.float8_e4m3fn).view(np.uint8)
    return words, np.ascontiguousarray(byte.astype(np.uint8).reshape(k // 512, 16, n))


def unpack_weight(words, scales):
    g, p, n, _ = words.shape
    vals = np.ascontiguousarray(words).view(ml_dtypes.float8_e4m3fn).astype(np.float64) * np.repeat(np.exp2(scales.astype(np.float64) - 127.0), 8, axis=1)[..., None]
    return vals.transpose(0, 1, 3, 2).reshape(g * 512, n)


K, T, D, S, V, N = 1024, 512, 6, 1536, 256, 512


def setup_inputs():
    n = np.random.standard_normal
    s = mx_kscale(K)[:, None]
    words, scales = pack_weight(n((K, N)) / np.sqrt(K) / s)
    return {
        "xT": (n((K, T)) * s).astype(np.float32),
        "w_words": words,
        "w_scales": scales,
        "b": (0.3 * n((N, 1))).astype(np.float32),
        "gate": np.tile(np.random.uniform(0.2, 1.0, (D, 1, V)) / np.sqrt(D), (1, N, 1)).astype(np.float32),
        "pos1": striped(np.random.permutation(T)[:V]),
        "pos2": striped(np.random.permutation(T)[:V]),
        "pos3": striped(np.random.permutation(T)[:V]),
        "pos4": striped(np.random.permutation(T)[:V]),
        "pos5": striped(np.random.permutation(T)[:V]),
        "pos6": striped(np.random.permutation(T)[:V]),
    }


def reference(xT, w_words, w_scales, b, gate, pos1, pos2, pos3, pos4, pos5, pos6):
    w = unpack_weight(w_words, w_scales)
    y = w.T @ mxq(f64(xT), 0, "e4m3")
    y = y + f64(b)
    return sum(f64(gate[d]) * y[:, unstriped(p)] for d, p in enumerate((pos1, pos2, pos3, pos4, pos5, pos6)))

@@ -1,0 +1,172 @@
+from contextlib import ExitStack
+
+import concourse.mybir as mybir
+
+K, T, D, V, N = 1024, 512, 6, 256, 512
+P = 128
+PACK = 4
+PASSES = K // (P * PACK)
+BLOCKS = N // P
+HALF = T // 2
+
+F32 = mybir.dt.float32
+BF16 = mybir.dt.bfloat16
+I32 = mybir.dt.int32
+U32 = mybir.dt.uint32
+U16 = mybir.dt.uint16
+U8 = mybir.dt.uint8
+FP8X4 = mybir.dt.float8_e4m3fn_x4
+
+ADD = mybir.AluOpType.add
+MULT = mybir.AluOpType.mult
+IDENTITY = mybir.ActivationFunctionType.Identity
+
+FLOPS = 2 * K * N * T + N * T + 2 * D * N * V
+
+VECTOR_NODES = 160
+
+
+def tile_picked_agg_lin_bias_sub_l_kernel(
+    tc, xT, w_words, w_scales, b, gate, pos1, pos2, pos3, pos4, pos5, pos6, out
+):
+    nc = tc.nc
+    with ExitStack() as ctx:
+        list_pool = ctx.enter_context(tc.tile_pool(name="lists", bufs=1))
+        keep = ctx.enter_context(tc.tile_pool(name="keep", bufs=1))
+        psum = ctx.enter_context(tc.psum_pool(name="psum", bufs=1))
+
+        positions = (pos1, pos2, pos3, pos4, pos5, pos6)
+        lists = [list_pool.tile([P, V // 16], U16, name=f"list{d}") for d in range(D)]
+
+        w_scale = keep.tile([P, PASSES, N], U8, align_bytes=64)
+        w_first = keep.tile([P, PASSES, P], U32, align_bytes=64)
+        w_rest = keep.tile([P, PASSES, N - P], U32, align_bytes=64)
+        x_pass0 = keep.tile([P, PACK, T], F32)
+        x_pass1 = [keep.tile([P, PACK, HALF], F32, name=f"x_pass1_{h}") for h in range(2)]
+        bias = keep.tile([P, BLOCKS], F32)
+        gates = [keep.tile([P, D, V], F32, name=f"gate{m}") for m in range(BLOCKS)]
+
+        warm = keep.tile([P, 1], F32)
+        warm_out = keep.tile([P, 1], F32)
+        nc.vector.memset(w_scale[:].bitcast(I32), 0)
+        nc.vector.memset(warm[:], 0.0)
+        nc.scalar.activation(warm_out[:], warm[:], IDENTITY)
+
+        w_view = w_words.rearrange("a p m r -> p a (m r)").bitcast(I32)
+        x_view = xT.rearrange("(a p j) n -> a p j n", a=PASSES, j=PACK)
+        gate_view = gate.rearrange("d (c p) v -> c p d v", p=P)
+
+        scale_view = w_scales.bitcast(I32).rearrange("a q m -> q a m")
+        for q in range(4):
+            nc.scalar.dma_start(
+                out=w_scale[32 * q : 32 * q + 4, :, :].bitcast(I32), in_=scale_view[4 * q : 4 * q + 4]
+            )
+        with nc.allow_non_contiguous_dma(reason="512 bias values, one to a partition and block"):
+            nc.scalar.dma_start(out=bias[:], in_=b.rearrange("(c p) o -> p (c o)", p=P))
+        nc.sync.dma_start(out=w_first[:].bitcast(I32), in_=w_view[:, :, 0:P])
+        nc.sync.dma_start(out=x_pass0[:], in_=x_view[0])
+        for h in range(2):
+            nc.sync.dma_start(out=x_pass1[h][:], in_=x_view[1, :, :, h * HALF : (h + 1) * HALF])
+        for d in range(D):
+            nc.sync.dma_start(lists[d][:], positions[d])
+        nc.sync.dma_start(out=gates[0][:, 0:3, :], in_=gate_view[0, :, 0:3, :])
+        nc.sync.dma_start(out=gates[0][:, 3:6, :], in_=gate_view[0, :, 3:6, :])
+        nc.sync.dma_start(out=w_rest[:].bitcast(I32), in_=w_view[:, :, P:N])
+        for m in range(1, BLOCKS):
+            nc.sync.dma_start(out=gates[m][:], in_=gate_view[m])
+
+        grouped = [
+            [keep.tile([P, HALF, PACK], BF16, align_bytes=64, name=f"grouped{a}{h}") for h in range(2)]
+            for a in range(PASSES)
+        ]
+        codes = keep.tile([P, PASSES, T], U32, align_bytes=64)
+        scales = keep.tile([P, PASSES, T], U8, align_bytes=64)
+
+        def interleave(a, h):
+            source = x_pass0[:, :, h * HALF : (h + 1) * HALF] if a == 0 else x_pass1[h][:]
+            for engine, lo, hi in ((nc.vector.tensor_copy, 0, VECTOR_NODES), (nc.scalar.copy, VECTOR_NODES, HALF)):
+                engine(
+                    out=grouped[a][h][:, lo:hi, :].rearrange("p (c i) t -> p c t i", i=4),
+                    in_=source[:, :, lo:hi].rearrange("p t (c i) -> p c t i", i=4),
+                )
+
+        def quantise(a, h):
+            nc.vector.quantize_mx(
+                out=codes[:, a, h * HALF : (h + 1) * HALF].bitcast(FP8X4),
+                scales=scales[:, a, h * HALF : (h + 1) * HALF],
+                in_=grouped[a][h][:].rearrange("p n j -> p (n j)"),
+            )
+
+        def multiply(acc, m, a, lo, hi):
+            words = w_first[:, a, :] if m == 0 else w_rest[:, a, (m - 1) * P : m * P]
+            nc.tensor.matmul_mx(
+                out=acc,
+                lhsT=words.bitcast(FP8X4),
+                lhsT_scale=w_scale[:, a, m * P : (m + 1) * P],
+                rhs=codes[:, a, lo:hi].bitcast(FP8X4),
+                rhs_scale=scales[:, a, lo:hi],
+                start=(a == 0),
+                stop=(a == PASSES - 1),
+            )
+
+        spans = ((0, HALF), (HALF, HALF + P), (HALF + P, T))
+        first = [psum.tile([P, hi - lo], F32, name=f"first{lo}") for lo, hi in spans]
+        y = [keep.tile([P, T], F32, name=f"y{m}") for m in range(BLOCKS)]
+
+        interleave(0, 0)
+        interleave(0, 1)
+        quantise(0, 0)
+        quantise(0, 1)
+        for a in range(PASSES):
+            for h in range(2):
+                if a == 1:
+                    interleave(a, h)
+                    quantise(a, h)
+                for acc, (lo, hi) in list(zip(first, spans))[h : 2 * h + 1]:
+                    multiply(acc[:], 0, a, lo, hi)
+        nc.scalar.activation(y[0][:, 0:HALF], first[0][:], IDENTITY, bias=bias[:, 0:1])
+        nc.scalar.activation(y[0][:, HALF : HALF + P], first[1][:], IDENTITY, bias=bias[:, 0:1])
+        nc.vector.tensor_scalar_add(y[0][:, HALF + P : T], first[2][:], bias[:, 0:1])
+
+        for m in range(1, BLOCKS):
+            acc = psum.tile([P, T], F32, name=f"acc{m}")
+            for a in range(PASSES):
+                multiply(acc[:], m, a, 0, T)
+            nc.scalar.activation(y[m][:], acc[:], IDENTITY, bias=bias[:, m : m + 1])
+
+        last = BLOCKS - 1
+        early_prod = keep.tile([P, last, D, V], F32)
+        early_part = keep.tile([P, last, 3, V], F32)
+        early_pair = keep.tile([P, last, V], F32)
+        early_total = keep.tile([P, last, V], F32)
+        last_prod = keep.tile([P, D, V], F32)
+        last_part = keep.tile([P, 3, V], F32)
+        last_pair = keep.tile([P, V], F32)
+        last_total = keep.tile([P, V], F32)
+
+        def gather(m, d):
+            result = last_prod[:, d, :] if m == last else early_prod[:, m, d, :]
+            nc.vector.tensor_tensor(result, y[m][:].indirect(lists[d][:]), gates[m][:, d, :], MULT)
+
+        def add(result, left, right):
+            nc.vector.tensor_tensor(result, left, right, ADD)
+
+        for m in range(last):
+            for d in range(D):
+                gather(m, d)
+
+        gather(last, 0)
+        add(early_part[:], early_prod[:, :, 0:3, :], early_prod[:, :, 3:6, :])
+        gather(last, 1)
+        add(early_pair[:], early_part[:, :, 0, :], early_part[:, :, 1, :])
+        gather(last, 2)
+        add(early_total[:], early_pair[:], early_part[:, :, 2, :])
+        nc.sync.dma_start(out=out[0 : last * P, :].rearrange("(c p) v -> p c v", p=P), in_=early_total[:])
+        gather(last, 3)
+        add(last_part[:, 0:2, :], last_prod[:, 0:2, :], last_prod[:, 2:4, :])
+        gather(last, 4)
+        add(last_pair[:], last_part[:, 0, :], last_part[:, 1, :])
+        gather(last, 5)
+        add(last_part[:, 2, :], last_pair[:], last_prod[:, 4, :])
+        add(last_total[:], last_part[:, 2, :], last_prod[:, 5, :])
+        nc.sync.dma_start(out=out[last * P : N, :], in_=last_total[:])

@@ -1,6 +1,7 @@
 from contextlib import ExitStack
 
 import concourse.mybir as mybir
+from concourse.masks import make_identity
 
 K, T, D, V, N = 1024, 512, 6, 256, 512
 P = 128
@@ -40,15 +41,19 @@ def tile_picked_agg_lin_bias_sub_l_kernel(
 
         w_scale = keep.tile([P, PASSES, N], U8, align_bytes=64)
         w_first = keep.tile([P, PASSES, P], U32, align_bytes=64)
-        w_rest = keep.tile([P, PASSES, N - P], U32, align_bytes=64)
+        w_second = keep.tile([P, PASSES, P], U32, align_bytes=64)
+        w_rest = keep.tile([P, PASSES, N - 2 * P], U32, align_bytes=64)
         x_pass0 = keep.tile([P, PACK, T], F32)
         x_pass1 = [keep.tile([P, PACK, HALF], F32, name=f"x_pass1_{h}") for h in range(2)]
+        bias_rows = keep.tile([P, P], F32)
+        identity = keep.tile([P, P], F32)
         bias = keep.tile([P, BLOCKS], F32)
         gates = [keep.tile([P, D, V], F32, name=f"gate{m}") for m in range(BLOCKS)]
 
         warm = keep.tile([P, 1], F32)
         warm_out = keep.tile([P, 1], F32)
         nc.vector.memset(w_scale[:].bitcast(I32), 0)
+        nc.vector.memset(bias_rows[:], 0.0)
         nc.vector.memset(warm[:], 0.0)
         nc.scalar.activation(warm_out[:], warm[:], IDENTITY)
 
@@ -61,17 +66,27 @@ def tile_picked_agg_lin_bias_sub_l_kernel(
             nc.scalar.dma_start(
                 out=w_scale[32 * q : 32 * q + 4, :, :].bitcast(I32), in_=scale_view[4 * q : 4 * q + 4]
             )
-        with nc.allow_non_contiguous_dma(reason="512 bias values, one to a partition and block"):
-            nc.scalar.dma_start(out=bias[:], in_=b.rearrange("(c p) o -> p (c o)", p=P))
+        nc.gpsimd.dma_start(out=bias_rows[0:BLOCKS, :], in_=b.rearrange("(c p) o -> c (p o)", p=P))
+        make_identity(nc, identity[:])
         nc.sync.dma_start(out=w_first[:].bitcast(I32), in_=w_view[:, :, 0:P])
         nc.sync.dma_start(out=x_pass0[:], in_=x_view[0])
         for h in range(2):
             nc.sync.dma_start(out=x_pass1[h][:], in_=x_view[1, :, :, h * HALF : (h + 1) * HALF])
-        for d in range(D):
-            nc.sync.dma_start(lists[d][:], positions[d])
-        nc.sync.dma_start(out=gates[0][:, 0:3, :], in_=gate_view[0, :, 0:3, :])
-        nc.sync.dma_start(out=gates[0][:, 3:6, :], in_=gate_view[0, :, 3:6, :])
-        nc.sync.dma_start(out=w_rest[:].bitcast(I32), in_=w_view[:, :, P:N])
+        def load_lists(lo, hi):
+            for d in range(lo, hi):
+                nc.sync.dma_start(lists[d][:], positions[d])
+
+        def load_first_gate(lo, hi):
+            nc.sync.dma_start(out=gates[0][:, lo:hi, :], in_=gate_view[0, :, lo:hi, :])
+
+        load_lists(0, 1)
+        load_first_gate(0, 2)
+        load_lists(1, 3)
+        nc.sync.dma_start(out=w_second[:].bitcast(I32), in_=w_view[:, :, P : 2 * P])
+        load_first_gate(2, 4)
+        load_lists(3, 6)
+        load_first_gate(4, 6)
+        nc.sync.dma_start(out=w_rest[:].bitcast(I32), in_=w_view[:, :, 2 * P : N])
         for m in range(1, BLOCKS):
             nc.sync.dma_start(out=gates[m][:], in_=gate_view[m])
 
@@ -98,7 +113,7 @@ def tile_picked_agg_lin_bias_sub_l_kernel(
             )
 
         def multiply(acc, m, a, lo, hi):
-            words = w_first[:, a, :] if m == 0 else w_rest[:, a, (m - 1) * P : m * P]
+            words = (w_first, w_second, w_rest, w_rest)[m][:, a, (m // 3) * P : (m // 3 + 1) * P]
             nc.tensor.matmul_mx(
                 out=acc,
                 lhsT=words.bitcast(FP8X4),
@@ -110,6 +125,10 @@ def tile_picked_agg_lin_bias_sub_l_kernel(
             )
 
         spans = ((0, HALF), (HALF, HALF + P), (HALF + P, T))
+        turned = psum.tile([P, P], F32)
+        nc.tensor.transpose(turned[:], bias_rows[:], identity[:])
+        nc.scalar.copy(bias[:], turned[:, 0:BLOCKS])
+
         first = [psum.tile([P, hi - lo], F32, name=f"first{lo}") for lo, hi in spans]
         y = [keep.tile([P, T], F32, name=f"y{m}") for m in range(BLOCKS)]
 

@@ -1,7 +1,6 @@
 from contextlib import ExitStack
 
 import concourse.mybir as mybir
-from concourse.masks import make_identity
 
 K, T, D, V, N = 1024, 512, 6, 256, 512
 P = 128
@@ -24,8 +23,6 @@ IDENTITY = mybir.ActivationFunctionType.Identity
 
 FLOPS = 2 * K * N * T + N * T + 2 * D * N * V
 
-VECTOR_NODES = 160
-
 
 def tile_picked_agg_lin_bias_sub_l_kernel(
     tc, xT, w_words, w_scales, b, gate, pos1, pos2, pos3, pos4, pos5, pos6, out
@@ -43,19 +40,22 @@ def tile_picked_agg_lin_bias_sub_l_kernel(
         w_first = keep.tile([P, PASSES, P], U32, align_bytes=64)
         w_second = keep.tile([P, PASSES, P], U32, align_bytes=64)
         w_rest = keep.tile([P, PASSES, N - 2 * P], U32, align_bytes=64)
-        x_pass0 = keep.tile([P, PACK, T], F32)
-        x_pass1 = [keep.tile([P, PACK, HALF], F32, name=f"x_pass1_{h}") for h in range(2)]
-        bias_rows = keep.tile([P, P], F32)
-        identity = keep.tile([P, P], F32)
-        bias = keep.tile([P, BLOCKS], F32)
+        chunks = (
+            (0, 0, 256, 160),
+            (0, 256, 512, 160),
+            (1, 0, 256, 160),
+            (1, 256, 384, 0),
+            (1, 384, 512, 128),
+        )
+        x_raw = [keep.tile([P, PACK, hi - lo], F32, name=f"x{a}_{lo}") for a, lo, hi, share in chunks]
+        first_bias = keep.tile([P, 1], F32)
+        rest_bias = keep.tile([P, BLOCKS - 1], F32)
         gates = [keep.tile([P, D, V], F32, name=f"gate{m}") for m in range(BLOCKS)]
 
         warm = keep.tile([P, 1], F32)
         warm_out = keep.tile([P, 1], F32)
-        nc.vector.memset(w_scale[:].bitcast(I32), 0)
-        nc.vector.memset(bias_rows[:], 0.0)
+        nc.gpsimd.memset(w_scale[:].bitcast(I32), 0)
         nc.vector.memset(warm[:], 0.0)
-        nc.scalar.activation(warm_out[:], warm[:], IDENTITY)
 
         w_view = w_words.rearrange("a p m r -> p a (m r)").bitcast(I32)
         x_view = xT.rearrange("(a p j) n -> a p j n", a=PASSES, j=PACK)
@@ -66,12 +66,13 @@ def tile_picked_agg_lin_bias_sub_l_kernel(
             nc.scalar.dma_start(
                 out=w_scale[32 * q : 32 * q + 4, :, :].bitcast(I32), in_=scale_view[4 * q : 4 * q + 4]
             )
-        nc.gpsimd.dma_start(out=bias_rows[0:BLOCKS, :], in_=b.rearrange("(c p) o -> c (p o)", p=P))
-        make_identity(nc, identity[:])
+        bias_view = b.rearrange("(c p) o -> p (c o)", p=P)
+        with nc.allow_non_contiguous_dma(reason="bias values, one to a partition"):
+            nc.scalar.dma_start(out=first_bias[:], in_=bias_view[:, 0:1])
+        nc.scalar.activation(warm_out[:], warm[:], IDENTITY)
         nc.sync.dma_start(out=w_first[:].bitcast(I32), in_=w_view[:, :, 0:P])
-        nc.sync.dma_start(out=x_pass0[:], in_=x_view[0])
-        for h in range(2):
-            nc.sync.dma_start(out=x_pass1[h][:], in_=x_view[1, :, :, h * HALF : (h + 1) * HALF])
+        for raw, (a, lo, hi, share) in zip(x_raw, chunks):
+            nc.sync.dma_start(out=raw[:], in_=x_view[a, :, :, lo:hi])
         def load_lists(lo, hi):
             for d in range(lo, hi):
                 nc.sync.dma_start(lists[d][:], positions[d])
@@ -82,34 +83,36 @@ def tile_picked_agg_lin_bias_sub_l_kernel(
         load_lists(0, 1)
         load_first_gate(0, 2)
         load_lists(1, 3)
-        nc.sync.dma_start(out=w_second[:].bitcast(I32), in_=w_view[:, :, P : 2 * P])
-        load_first_gate(2, 4)
+        load_first_gate(2, 6)
         load_lists(3, 6)
-        load_first_gate(4, 6)
+        nc.sync.dma_start(out=w_second[:].bitcast(I32), in_=w_view[:, :, P : 2 * P])
+        with nc.allow_non_contiguous_dma(reason="bias values, one to a partition and block"):
+            nc.sync.dma_start(out=rest_bias[:], in_=bias_view[:, 1:BLOCKS])
         nc.sync.dma_start(out=w_rest[:].bitcast(I32), in_=w_view[:, :, 2 * P : N])
         for m in range(1, BLOCKS):
             nc.sync.dma_start(out=gates[m][:], in_=gate_view[m])
 
         grouped = [
-            [keep.tile([P, HALF, PACK], BF16, align_bytes=64, name=f"grouped{a}{h}") for h in range(2)]
-            for a in range(PASSES)
+            keep.tile([P, hi - lo, PACK], BF16, align_bytes=64, name=f"grouped{a}_{lo}") for a, lo, hi, share in chunks
         ]
         codes = keep.tile([P, PASSES, T], U32, align_bytes=64)
         scales = keep.tile([P, PASSES, T], U8, align_bytes=64)
 
-        def interleave(a, h):
-            source = x_pass0[:, :, h * HALF : (h + 1) * HALF] if a == 0 else x_pass1[h][:]
-            for engine, lo, hi in ((nc.vector.tensor_copy, 0, VECTOR_NODES), (nc.scalar.copy, VECTOR_NODES, HALF)):
-                engine(
-                    out=grouped[a][h][:, lo:hi, :].rearrange("p (c i) t -> p c t i", i=4),
-                    in_=source[:, :, lo:hi].rearrange("p t (c i) -> p c t i", i=4),
-                )
+        def interleave(c):
+            a, lo, hi, share = chunks[c]
+            for engine, start, end in ((nc.vector.tensor_copy, 0, share), (nc.scalar.copy, share, hi - lo)):
+                if end > start:
+                    engine(
+                        out=grouped[c][:, start:end, :].rearrange("p (c i) t -> p c t i", i=4),
+                        in_=x_raw[c][:, :, start:end].rearrange("p t (c i) -> p c t i", i=4),
+                    )
 
-        def quantise(a, h):
+        def quantise(c):
+            a, lo, hi, share = chunks[c]
             nc.vector.quantize_mx(
-                out=codes[:, a, h * HALF : (h + 1) * HALF].bitcast(FP8X4),
-                scales=scales[:, a, h * HALF : (h + 1) * HALF],
-                in_=grouped[a][h][:].rearrange("p n j -> p (n j)"),
+                out=codes[:, a, lo:hi].bitcast(FP8X4),
+                scales=scales[:, a, lo:hi],
+                in_=grouped[c][:].rearrange("p n j -> p (n j)"),
             )
 
         def multiply(acc, m, a, lo, hi):
@@ -125,33 +128,33 @@ def tile_picked_agg_lin_bias_sub_l_kernel(
             )
 
         spans = ((0, HALF), (HALF, HALF + P), (HALF + P, T))
-        turned = psum.tile([P, P], F32)
-        nc.tensor.transpose(turned[:], bias_rows[:], identity[:])
-        nc.scalar.copy(bias[:], turned[:, 0:BLOCKS])
-
         first = [psum.tile([P, hi - lo], F32, name=f"first{lo}") for lo, hi in spans]
         y = [keep.tile([P, T], F32, name=f"y{m}") for m in range(BLOCKS)]
 
-        interleave(0, 0)
-        interleave(0, 1)
-        quantise(0, 0)
-        quantise(0, 1)
-        for a in range(PASSES):
-            for h in range(2):
-                if a == 1:
-                    interleave(a, h)
-                    quantise(a, h)
-                for acc, (lo, hi) in list(zip(first, spans))[h : 2 * h + 1]:
-                    multiply(acc[:], 0, a, lo, hi)
-        nc.scalar.activation(y[0][:, 0:HALF], first[0][:], IDENTITY, bias=bias[:, 0:1])
-        nc.scalar.activation(y[0][:, HALF : HALF + P], first[1][:], IDENTITY, bias=bias[:, 0:1])
-        nc.vector.tensor_scalar_add(y[0][:, HALF + P : T], first[2][:], bias[:, 0:1])
+        interleave(0)
+        interleave(1)
+        quantise(0)
+        quantise(1)
+        for acc, (lo, hi) in zip(first, spans):
+            multiply(acc[:], 0, 0, lo, hi)
+        interleave(2)
+        quantise(2)
+        multiply(first[0][:], 0, 1, *spans[0])
+        interleave(3)
+        interleave(4)
+        quantise(3)
+        multiply(first[1][:], 0, 1, *spans[1])
+        quantise(4)
+        multiply(first[2][:], 0, 1, *spans[2])
+        nc.scalar.activation(y[0][:, 0:HALF], first[0][:], IDENTITY, bias=first_bias[:])
+        nc.scalar.activation(y[0][:, HALF : HALF + P], first[1][:], IDENTITY, bias=first_bias[:])
+        nc.vector.tensor_scalar_add(y[0][:, HALF + P : T], first[2][:], first_bias[:])
 
         for m in range(1, BLOCKS):
             acc = psum.tile([P, T], F32, name=f"acc{m}")
             for a in range(PASSES):
                 multiply(acc[:], m, a, 0, T)
-            nc.scalar.activation(y[m][:], acc[:], IDENTITY, bias=bias[:, m : m + 1])
+            nc.scalar.activation(y[m][:], acc[:], IDENTITY, bias=rest_bias[:, m - 1 : m])
 
         last = BLOCKS - 1
         early_prod = keep.tile([P, last, D, V], F32)

@@ -44,10 +44,11 @@ def tile_picked_agg_lin_bias_sub_l_kernel(
             (0, 0, 256, 160),
             (0, 256, 512, 160),
             (1, 0, 256, 160),
-            (1, 256, 384, 0),
-            (1, 384, 512, 128),
+            (1, 256, 512, 144),
         )
-        x_raw = [keep.tile([P, PACK, hi - lo], F32, name=f"x{a}_{lo}") for a, lo, hi, share in chunks]
+        x_first = keep.tile([P, PACK, T], F32)
+        x_second = [keep.tile([P, PACK, HALF], F32, name=f"x_second{h}") for h in range(2)]
+        x_raw = [x_first[:, :, 0:HALF], x_first[:, :, HALF:T], x_second[0][:], x_second[1][:]]
         first_bias = keep.tile([P, 1], F32)
         rest_bias = keep.tile([P, BLOCKS - 1], F32)
         gates = [keep.tile([P, D, V], F32, name=f"gate{m}") for m in range(BLOCKS)]
@@ -70,27 +71,31 @@ def tile_picked_agg_lin_bias_sub_l_kernel(
         with nc.allow_non_contiguous_dma(reason="bias values, one to a partition"):
             nc.scalar.dma_start(out=first_bias[:], in_=bias_view[:, 0:1])
         nc.scalar.activation(warm_out[:], warm[:], IDENTITY)
+        nc.sync.dma_start(out=x_first[:], in_=x_view[0])
+        for h in range(2):
+            nc.sync.dma_start(out=x_second[h][:], in_=x_view[1, :, :, h * HALF : (h + 1) * HALF])
         nc.sync.dma_start(out=w_first[:].bitcast(I32), in_=w_view[:, :, 0:P])
-        for raw, (a, lo, hi, share) in zip(x_raw, chunks):
-            nc.sync.dma_start(out=raw[:], in_=x_view[a, :, :, lo:hi])
         def load_lists(lo, hi):
             for d in range(lo, hi):
                 nc.sync.dma_start(lists[d][:], positions[d])
 
-        def load_first_gate(lo, hi):
-            nc.sync.dma_start(out=gates[0][:, lo:hi, :], in_=gate_view[0, :, lo:hi, :])
+        def load_gate(m, lo, hi):
+            nc.sync.dma_start(out=gates[m][:, lo:hi, :], in_=gate_view[m, :, lo:hi, :])
 
         load_lists(0, 1)
-        load_first_gate(0, 2)
+        load_gate(0, 0, 2)
         load_lists(1, 3)
-        load_first_gate(2, 6)
+        load_gate(0, 2, 6)
         load_lists(3, 6)
         nc.sync.dma_start(out=w_second[:].bitcast(I32), in_=w_view[:, :, P : 2 * P])
         with nc.allow_non_contiguous_dma(reason="bias values, one to a partition and block"):
             nc.sync.dma_start(out=rest_bias[:], in_=bias_view[:, 1:BLOCKS])
+        load_gate(1, 0, 2)
+        load_gate(1, 2, 6)
         nc.sync.dma_start(out=w_rest[:].bitcast(I32), in_=w_view[:, :, 2 * P : N])
-        for m in range(1, BLOCKS):
-            nc.sync.dma_start(out=gates[m][:], in_=gate_view[m])
+        load_gate(2, 0, 3)
+        load_gate(2, 3, 6)
+        load_gate(3, 0, 6)
 
         grouped = [
             keep.tile([P, hi - lo, PACK], BF16, align_bytes=64, name=f"grouped{a}_{lo}") for a, lo, hi, share in chunks
@@ -141,14 +146,12 @@ def tile_picked_agg_lin_bias_sub_l_kernel(
         quantise(2)
         multiply(first[0][:], 0, 1, *spans[0])
         interleave(3)
-        interleave(4)
         quantise(3)
-        multiply(first[1][:], 0, 1, *spans[1])
-        quantise(4)
-        multiply(first[2][:], 0, 1, *spans[2])
+        for acc, (lo, hi) in list(zip(first, spans))[1:]:
+            multiply(acc[:], 0, 1, lo, hi)
         nc.scalar.activation(y[0][:, 0:HALF], first[0][:], IDENTITY, bias=first_bias[:])
-        nc.scalar.activation(y[0][:, HALF : HALF + P], first[1][:], IDENTITY, bias=first_bias[:])
-        nc.vector.tensor_scalar_add(y[0][:, HALF + P : T], first[2][:], first_bias[:])
+        nc.vector.tensor_scalar_add(y[0][:, HALF : HALF + P], first[1][:], first_bias[:])
+        nc.scalar.activation(y[0][:, HALF + P : T], first[2][:], IDENTITY, bias=first_bias[:])
 
         for m in range(1, BLOCKS):
             acc = psum.tile([P, T], F32, name=f"acc{m}")
@@ -166,9 +169,10 @@ def tile_picked_agg_lin_bias_sub_l_kernel(
         last_pair = keep.tile([P, V], F32)
         last_total = keep.tile([P, V], F32)
 
-        def gather(m, d):
-            result = last_prod[:, d, :] if m == last else early_prod[:, m, d, :]
-            nc.vector.tensor_tensor(result, y[m][:].indirect(lists[d][:]), gates[m][:, d, :], MULT)
+        def gather(m, d, lo=0, hi=V):
+            result = last_prod[:, d, lo:hi] if m == last else early_prod[:, m, d, lo:hi]
+            offsets = lists[d][:] if hi - lo == V else lists[d][:, lo // 16 : hi // 16]
+            nc.vector.tensor_tensor(result, y[m][:].indirect(offsets), gates[m][:, d, lo:hi], MULT)
 
         def add(result, left, right):
             nc.vector.tensor_tensor(result, left, right, ADD)
@@ -182,13 +186,16 @@ def tile_picked_agg_lin_bias_sub_l_kernel(
         gather(last, 1)
         add(early_pair[:], early_part[:, :, 0, :], early_part[:, :, 1, :])
         gather(last, 2)
+        gather(last, 3)
         add(early_total[:], early_pair[:], early_part[:, :, 2, :])
         nc.sync.dma_start(out=out[0 : last * P, :].rearrange("(c p) v -> p c v", p=P), in_=early_total[:])
-        gather(last, 3)
         add(last_part[:, 0:2, :], last_prod[:, 0:2, :], last_prod[:, 2:4, :])
         gather(last, 4)
         add(last_pair[:], last_part[:, 0, :], last_part[:, 1, :])
-        gather(last, 5)
+        gather(last, 5, 0, V // 2)
         add(last_part[:, 2, :], last_pair[:], last_prod[:, 4, :])
-        add(last_total[:], last_part[:, 2, :], last_prod[:, 5, :])
+        gather(last, 5, V // 2, V)
+        for lo in (0, V // 2):
+            hi = lo + V // 2
+            add(last_total[:, lo:hi], last_part[:, 2, lo:hi], last_prod[:, 5, lo:hi])
         nc.sync.dma_start(out=out[last * P : N, :], in_=last_total[:])

from contextlib import ExitStack

import concourse.mybir as mybir

K, T, D, V, N = 1024, 512, 6, 256, 512
P = 128
PACK = 4
PASSES = K // (P * PACK)
BLOCKS = N // P
HALF = T // 2

F32 = mybir.dt.float32
BF16 = mybir.dt.bfloat16
I32 = mybir.dt.int32
U32 = mybir.dt.uint32
U16 = mybir.dt.uint16
U8 = mybir.dt.uint8
FP8X4 = mybir.dt.float8_e4m3fn_x4

ADD = mybir.AluOpType.add
MULT = mybir.AluOpType.mult
IDENTITY = mybir.ActivationFunctionType.Identity

FLOPS = 2 * K * N * T + N * T + 2 * D * N * V


def tile_picked_agg_lin_bias_sub_l_kernel(
    tc, xT, w_words, w_scales, b, gate, pos1, pos2, pos3, pos4, pos5, pos6, out
):
    nc = tc.nc
    with ExitStack() as ctx:
        list_pool = ctx.enter_context(tc.tile_pool(name="lists", bufs=1))
        keep = ctx.enter_context(tc.tile_pool(name="keep", bufs=1))
        psum = ctx.enter_context(tc.psum_pool(name="psum", bufs=1))

        positions = (pos1, pos2, pos3, pos4, pos5, pos6)
        lists = [list_pool.tile([P, V // 16], U16, name=f"list{d}") for d in range(D)]

        w_scale = keep.tile([P, PASSES, N], U8, align_bytes=64)
        w_first = keep.tile([P, PASSES, P], U32, align_bytes=64)
        w_second = keep.tile([P, PASSES, P], U32, align_bytes=64)
        w_rest = keep.tile([P, PASSES, N - 2 * P], U32, align_bytes=64)
        chunks = (
            (0, 0, 256, 160),
            (0, 256, 512, 160),
            (1, 0, 256, 160),
            (1, 256, 512, 144),
        )
        x_first = keep.tile([P, PACK, T], F32)
        x_second = [keep.tile([P, PACK, HALF], F32, name=f"x_second{h}") for h in range(2)]
        x_raw = [x_first[:, :, 0:HALF], x_first[:, :, HALF:T], x_second[0][:], x_second[1][:]]
        first_bias = keep.tile([P, 1], F32)
        rest_bias = keep.tile([P, BLOCKS - 1], F32)
        gates = [keep.tile([P, D, V], F32, name=f"gate{m}") for m in range(BLOCKS)]

        warm = keep.tile([P, 1], F32)
        warm_out = keep.tile([P, 1], F32)
        nc.gpsimd.memset(w_scale[:].bitcast(I32), 0)
        nc.vector.memset(warm[:], 0.0)

        w_view = w_words.rearrange("a p m r -> p a (m r)").bitcast(I32)
        x_view = xT.rearrange("(a p j) n -> a p j n", a=PASSES, j=PACK)
        gate_view = gate.rearrange("d (c p) v -> c p d v", p=P)

        scale_view = w_scales.bitcast(I32).rearrange("a q m -> q a m")
        for q in range(4):
            nc.scalar.dma_start(
                out=w_scale[32 * q : 32 * q + 4, :, :].bitcast(I32), in_=scale_view[4 * q : 4 * q + 4]
            )
        bias_view = b.rearrange("(c p) o -> p (c o)", p=P)
        with nc.allow_non_contiguous_dma(reason="bias values, one to a partition"):
            nc.scalar.dma_start(out=first_bias[:], in_=bias_view[:, 0:1])
        nc.scalar.activation(warm_out[:], warm[:], IDENTITY)
        nc.sync.dma_start(out=x_first[:], in_=x_view[0])
        for h in range(2):
            nc.sync.dma_start(out=x_second[h][:], in_=x_view[1, :, :, h * HALF : (h + 1) * HALF])
        nc.sync.dma_start(out=w_first[:].bitcast(I32), in_=w_view[:, :, 0:P])
        def load_lists(lo, hi):
            for d in range(lo, hi):
                nc.sync.dma_start(lists[d][:], positions[d])

        def load_gate(m, lo, hi):
            nc.sync.dma_start(out=gates[m][:, lo:hi, :], in_=gate_view[m, :, lo:hi, :])

        load_lists(0, 1)
        load_gate(0, 0, 2)
        load_lists(1, 3)
        load_gate(0, 2, 6)
        load_lists(3, 6)
        nc.sync.dma_start(out=w_second[:].bitcast(I32), in_=w_view[:, :, P : 2 * P])
        with nc.allow_non_contiguous_dma(reason="bias values, one to a partition and block"):
            nc.sync.dma_start(out=rest_bias[:], in_=bias_view[:, 1:BLOCKS])
        load_gate(1, 0, 2)
        load_gate(1, 2, 6)
        nc.sync.dma_start(out=w_rest[:].bitcast(I32), in_=w_view[:, :, 2 * P : N])
        load_gate(2, 0, 3)
        load_gate(2, 3, 6)
        load_gate(3, 0, 6)

        grouped = [
            keep.tile([P, hi - lo, PACK], BF16, align_bytes=64, name=f"grouped{a}_{lo}") for a, lo, hi, share in chunks
        ]
        codes = keep.tile([P, PASSES, T], U32, align_bytes=64)
        scales = keep.tile([P, PASSES, T], U8, align_bytes=64)

        def interleave(c):
            a, lo, hi, share = chunks[c]
            for engine, start, end in ((nc.vector.tensor_copy, 0, share), (nc.scalar.copy, share, hi - lo)):
                if end > start:
                    engine(
                        out=grouped[c][:, start:end, :].rearrange("p (c i) t -> p c t i", i=4),
                        in_=x_raw[c][:, :, start:end].rearrange("p t (c i) -> p c t i", i=4),
                    )

        def quantise(c):
            a, lo, hi, share = chunks[c]
            nc.vector.quantize_mx(
                out=codes[:, a, lo:hi].bitcast(FP8X4),
                scales=scales[:, a, lo:hi],
                in_=grouped[c][:].rearrange("p n j -> p (n j)"),
            )

        def multiply(acc, m, a, lo, hi):
            words = (w_first, w_second, w_rest, w_rest)[m][:, a, (m // 3) * P : (m // 3 + 1) * P]
            nc.tensor.matmul_mx(
                out=acc,
                lhsT=words.bitcast(FP8X4),
                lhsT_scale=w_scale[:, a, m * P : (m + 1) * P],
                rhs=codes[:, a, lo:hi].bitcast(FP8X4),
                rhs_scale=scales[:, a, lo:hi],
                start=(a == 0),
                stop=(a == PASSES - 1),
            )

        spans = ((0, HALF), (HALF, HALF + P), (HALF + P, T))
        first = [psum.tile([P, hi - lo], F32, name=f"first{lo}") for lo, hi in spans]
        y = [keep.tile([P, T], F32, name=f"y{m}") for m in range(BLOCKS)]

        interleave(0)
        interleave(1)
        quantise(0)
        quantise(1)
        for acc, (lo, hi) in zip(first, spans):
            multiply(acc[:], 0, 0, lo, hi)
        interleave(2)
        quantise(2)
        multiply(first[0][:], 0, 1, *spans[0])
        interleave(3)
        quantise(3)
        for acc, (lo, hi) in list(zip(first, spans))[1:]:
            multiply(acc[:], 0, 1, lo, hi)
        nc.scalar.activation(y[0][:, 0:HALF], first[0][:], IDENTITY, bias=first_bias[:])
        nc.vector.tensor_scalar_add(y[0][:, HALF : HALF + P], first[1][:], first_bias[:])
        nc.scalar.activation(y[0][:, HALF + P : T], first[2][:], IDENTITY, bias=first_bias[:])

        for m in range(1, BLOCKS):
            acc = psum.tile([P, T], F32, name=f"acc{m}")
            for a in range(PASSES):
                multiply(acc[:], m, a, 0, T)
            nc.scalar.activation(y[m][:], acc[:], IDENTITY, bias=rest_bias[:, m - 1 : m])

        last = BLOCKS - 1
        early_prod = keep.tile([P, last, D, V], F32)
        early_part = keep.tile([P, last, 3, V], F32)
        early_pair = keep.tile([P, last, V], F32)
        early_total = keep.tile([P, last, V], F32)
        last_prod = keep.tile([P, D, V], F32)
        last_part = keep.tile([P, 3, V], F32)
        last_pair = keep.tile([P, V], F32)
        last_total = keep.tile([P, V], F32)

        def gather(m, d, lo=0, hi=V):
            result = last_prod[:, d, lo:hi] if m == last else early_prod[:, m, d, lo:hi]
            offsets = lists[d][:] if hi - lo == V else lists[d][:, lo // 16 : hi // 16]
            nc.vector.tensor_tensor(result, y[m][:].indirect(offsets), gates[m][:, d, lo:hi], MULT)

        def add(result, left, right):
            nc.vector.tensor_tensor(result, left, right, ADD)

        for m in range(last):
            for d in range(D):
                gather(m, d)

        gather(last, 0)
        add(early_part[:], early_prod[:, :, 0:3, :], early_prod[:, :, 3:6, :])
        gather(last, 1)
        add(early_pair[:], early_part[:, :, 0, :], early_part[:, :, 1, :])
        gather(last, 2)
        gather(last, 3)
        add(early_total[:], early_pair[:], early_part[:, :, 2, :])
        nc.sync.dma_start(out=out[0 : last * P, :].rearrange("(c p) v -> p c v", p=P), in_=early_total[:])
        add(last_part[:, 0:2, :], last_prod[:, 0:2, :], last_prod[:, 2:4, :])
        gather(last, 4)
        add(last_pair[:], last_part[:, 0, :], last_part[:, 1, :])
        gather(last, 5, 0, V // 2)
        add(last_part[:, 2, :], last_pair[:], last_prod[:, 4, :])
        gather(last, 5, V // 2, V)
        for lo in (0, V // 2):
            hi = lo + V // 2
            add(last_total[:, lo:hi], last_part[:, 2, lo:hi], last_prod[:, 5, lo:hi])
        nc.sync.dma_start(out=out[last * P : N, :], in_=last_total[:])
